import numpy as np
import ml_dtypes


def mxq(x, axis, fmt="e4m3"):
    dtype, down = {"e4m3": (ml_dtypes.float8_e4m3fn, 7), "e5m2": (ml_dtypes.float8_e5m2, 14)}[fmt]
    v = np.moveaxis(np.asarray(x, np.float32).astype(ml_dtypes.bfloat16).astype(np.float64), axis, -1)
    blocks = v.reshape(v.shape[:-1] + (-1, 32))
    amax = np.abs(blocks).max(-1, keepdims=True)
    byte = np.maximum(np.where(amax > 0, np.frexp(amax)[1] - 1 + 127, 0) - down, 1)
    scale = np.exp2(byte - 127.0)
    codes = (blocks / scale).astype(np.float32).astype(dtype).astype(np.float64)
    return np.moveaxis((codes * scale).reshape(v.shape), -1, axis)


WIDE = False


def mx_kscale(k):
    if not WIDE:
        return np.ones(k)
    levels = np.array([10, -10, 5, -5, 0])
    if k % 512:
        return np.exp2(np.random.permutation(np.resize(levels, k // 32))).repeat(32)
    a = np.empty((k // 512, 16))
    for p in range(k // 512):
        a[p, :8] = np.random.permutation(np.resize(levels, 8))
        for g in range(8):
            far = levels[np.abs(levels - a[p, g]) >= 10]
            a[p, g + 8] = far[np.random.randint(len(far))]
    return np.exp2(a.ravel()).repeat(32)


def f64(x):
    return np.asarray(x).astype(np.float64)


def striped(idx):
    return np.tile(idx.reshape(-1, 16).T, (8, 1)).astype(np.uint16)


def unstriped(offs):
    return offs[:16].T.reshape(-1).astype(np.int64)


def pack_weight(w):
    k, n = w.shape
    w = f64(np.asarray(w, np.float32).astype(ml_dtypes.bfloat16)).reshape(k // 32, 32, n)
    amax = np.abs(w).max(1)
    byte = np.clip(np.where(amax > 0, np.frexp(amax)[1] - 1 + 127 - 7, 1), 1, 254)
    scaled = (w * np.exp2(127.0 - byte)[:, None, :]).reshape(k, n).astype(np.float32)
    words = np.ascontiguousarray(scaled.reshape(k // 512, 128, 4, n).transpose(0, 1, 3, 2)).astype(ml_dtypes.float8_e4m3fn).view(np.uint8)
    return words, np.ascontiguousarray(byte.astype(np.uint8).reshape(k // 512, 16, n))


def unpack_weight(words, scales):
    g, p, n, _ = words.shape
    vals = np.ascontiguousarray(words).view(ml_dtypes.float8_e4m3fn).astype(np.float64) * np.repeat(np.exp2(scales.astype(np.float64) - 127.0), 8, axis=1)[..., None]
    return vals.transpose(0, 1, 3, 2).reshape(g * 512, n)


K, T, S, N, U = 1024, 2048, 1024, 128, 2048


def setup_inputs():
    n = np.random.standard_normal
    s = mx_kscale(K)[:, None]
    packed_xT = pack_weight(n((K, T)) * s)
    return {
        "x_words": packed_xT[0],
        "x_scales": packed_xT[1],
        "mem": n((N, U)).astype(np.float32),
        "w1": (n((K, N)) / np.sqrt(K) / s).astype(np.float32),
        "offs": striped(np.random.permutation(T)[:S]),
        "slot": striped(np.random.permutation(U)[:S]),
    }


def reference(x_words, x_scales, mem, w1, offs, slot):
    xq = unpack_weight(x_words, x_scales)[:, unstriped(offs)]
    y = mxq(f64(w1), 0, "e4m3").T @ xq
    out = f64(mem).copy()
    out[:, unstriped(slot)] = np.minimum(f64(mem)[:, unstriped(slot)], y)
    return out

@@ -1,0 +1,87 @@
+from contextlib import ExitStack
+
+import concourse.mybir as mybir
+
+K, T, S, N, U = 1024, 2048, 1024, 128, 2048
+FLOPS = 2 * K * S * N
+
+F32 = mybir.dt.float32
+BF16 = mybir.dt.bfloat16
+I32 = mybir.dt.int32
+U32 = mybir.dt.uint32
+U16 = mybir.dt.uint16
+U8 = mybir.dt.uint8
+FP8X4 = mybir.dt.float8_e4m3fn_x4
+
+P = 128
+PACK = 4
+PASSES = K // (P * PACK)
+BANK = 512
+
+
+def tile_picked_idxput_min_p_kernel(tc, x_words, x_scales, mem, w1, offs, slot, out):
+    nc = tc.nc
+    with ExitStack() as ctx:
+        keep = ctx.enter_context(tc.tile_pool(name="keep", bufs=1))
+        psum = ctx.enter_context(tc.psum_pool(name="psum", bufs=1))
+
+        offs_sb = keep.tile([P, S // 16], U16, name="offs_sb")
+        slot_sb = keep.tile([P, S // 16], U16, name="slot_sb")
+        scales = keep.tile([P, T], U8, name="scales", align_bytes=64)
+        words = [keep.tile([P, T], I32, name=f"words{z}", align_bytes=64) for z in range(PASSES)]
+        store = keep.tile([P, U], F32, name="store", align_bytes=64)
+        w_raw = [keep.tile([P, PACK, N], F32, name=f"w_raw{z}", align_bytes=64) for z in range(PASSES)]
+
+        nc.vector.memset(scales[:].bitcast(I32), 0)
+        nc.sync.dma_start(offs_sb[:], offs)
+        nc.sync.dma_start(w_raw[0][:], w1[0:512, :].rearrange("(p j) n -> p j n", j=PACK))
+        for q in range(4):
+            nc.sync.dma_start(
+                scales[32 * q : 32 * q + 4 * PASSES, :].bitcast(I32),
+                x_scales[:, 4 * q : 4 * q + 4, :].bitcast(I32),
+            )
+        for z in range(PASSES):
+            nc.sync.dma_start(words[z][:], x_words[z].rearrange("p n t -> p (n t)").bitcast(I32))
+        nc.sync.dma_start(w_raw[1][:], w1[512:1024, :].rearrange("(p j) n -> p j n", j=PACK))
+        nc.sync.dma_start(store[:], mem)
+        nc.sync.dma_start(slot_sb[:], slot)
+
+        w_bf = keep.tile([P, PASSES, N, PACK], BF16, name="w_bf", align_bytes=64)
+        for z in range(PASSES):
+            nc.scalar.copy(w_bf[:, z], w_raw[z][:].rearrange("p j n -> p n j"))
+
+        picked_scales = keep.tile([P, S], U8, name="picked_scales", align_bytes=64)
+        nc.vector.tensor_copy(picked_scales[:], scales[:].indirect(offs_sb[:]))
+        picked = [keep.tile([P, S], U32, name=f"picked{z}", align_bytes=64) for z in range(PASSES)]
+        for z in range(PASSES):
+            nc.vector.tensor_copy(picked[z][:], words[z][:].bitcast(U32).indirect(offs_sb[:]))
+
+        w_codes = keep.tile([P, PASSES * N], U32, name="w_codes", align_bytes=64)
+        w_scales = keep.tile([P, PASSES * N], U8, name="w_scales", align_bytes=64)
+        nc.vector.quantize_mx(
+            out=w_codes[:].bitcast(FP8X4),
+            scales=w_scales[:],
+            in_=w_bf[:].rearrange("p z n j -> p (z n j)"),
+        )
+
+        old = keep.tile([P, S], F32, name="old", align_bytes=64)
+        nc.vector.tensor_copy(old[:], store[:].indirect(slot_sb[:]))
+
+        new = keep.tile([P, S], F32, name="new", align_bytes=64)
+        for h in range(S // BANK):
+            cols = slice(h * BANK, (h + 1) * BANK)
+            acc = psum.tile([P, BANK], F32, name=f"acc{h}")
+            for z in range(PASSES):
+                nc.tensor.matmul_mx(
+                    out=acc[:],
+                    lhsT=w_codes[:, z * N : (z + 1) * N].bitcast(FP8X4),
+                    lhsT_scale=w_scales[:, z * N : (z + 1) * N],
+                    rhs=picked[z][:, cols].bitcast(FP8X4),
+                    rhs_scale=picked_scales[4 * z : P, cols],
+                    start=(z == 0),
+                    stop=(z == PASSES - 1),
+                )
+            nc.vector.tensor_tensor(new[:, cols], acc[:], old[:, cols], mybir.AluOpType.min)
+
+        nc.vector.tensor_copy(store[:].indirect(slot_sb[:]), new[:])
+        nc.sync.dma_start(out, store[:])

@@ -33,18 +33,18 @@ def tile_picked_idxput_min_p_kernel(tc, x_words, x_scales, mem, w1, offs, slot, 
         w_raw = [keep.tile([P, PACK, N], F32, name=f"w_raw{z}", align_bytes=64) for z in range(PASSES)]
 
         nc.vector.memset(scales[:].bitcast(I32), 0)
+        planes = keep.tile([P, PASSES * S], U8, name="planes", align_bytes=64)
+        nc.vector.memset(planes[:].bitcast(I32), 0)
         nc.sync.dma_start(offs_sb[:], offs)
+        nc.sync.dma_start(slot_sb[:], slot)
         nc.sync.dma_start(w_raw[0][:], w1[0:512, :].rearrange("(p j) n -> p j n", j=PACK))
-        for q in range(4):
-            nc.sync.dma_start(
-                scales[32 * q : 32 * q + 4 * PASSES, :].bitcast(I32),
-                x_scales[:, 4 * q : 4 * q + 4, :].bitcast(I32),
-            )
+        nc.sync.dma_start(
+            scales[0:P:4, :].bitcast(I32), x_scales.rearrange("z g c -> g z c").bitcast(I32)
+        )
         for z in range(PASSES):
             nc.sync.dma_start(words[z][:], x_words[z].rearrange("p n t -> p (n t)").bitcast(I32))
         nc.sync.dma_start(w_raw[1][:], w1[512:1024, :].rearrange("(p j) n -> p j n", j=PACK))
         nc.sync.dma_start(store[:], mem)
-        nc.sync.dma_start(slot_sb[:], slot)
 
         w_bf = keep.tile([P, PASSES, N, PACK], BF16, name="w_bf", align_bytes=64)
         for z in range(PASSES):
@@ -52,6 +52,11 @@ def tile_picked_idxput_min_p_kernel(tc, x_words, x_scales, mem, w1, offs, slot, 
 
         picked_scales = keep.tile([P, S], U8, name="picked_scales", align_bytes=64)
         nc.vector.tensor_copy(picked_scales[:], scales[:].indirect(offs_sb[:]))
+        for q in range(4):
+            nc.scalar.dma_start(
+                planes[32 * q : 32 * q + 4, :].bitcast(I32).rearrange("r (z c) -> r z c", z=PASSES),
+                picked_scales[32 * q : 32 * q + 32 : 4, :].bitcast(I32),
+            )
         picked = [keep.tile([P, S], U32, name=f"picked{z}", align_bytes=64) for z in range(PASSES)]
         for z in range(PASSES):
             nc.vector.tensor_copy(picked[z][:], words[z][:].bitcast(U32).indirect(offs_sb[:]))
@@ -68,20 +73,22 @@ def tile_picked_idxput_min_p_kernel(tc, x_words, x_scales, mem, w1, offs, slot, 
         nc.vector.tensor_copy(old[:], store[:].indirect(slot_sb[:]))
 
         new = keep.tile([P, S], F32, name="new", align_bytes=64)
-        for h in range(S // BANK):
-            cols = slice(h * BANK, (h + 1) * BANK)
-            acc = psum.tile([P, BANK], F32, name=f"acc{h}")
-            for z in range(PASSES):
+        acc = [psum.tile([P, BANK], F32, name=f"acc{h}") for h in range(S // BANK)]
+        for z in range(PASSES):
+            for h in range(S // BANK):
+                cols = slice(h * BANK, (h + 1) * BANK)
                 nc.tensor.matmul_mx(
-                    out=acc[:],
+                    out=acc[h][:],
                     lhsT=w_codes[:, z * N : (z + 1) * N].bitcast(FP8X4),
                     lhsT_scale=w_scales[:, z * N : (z + 1) * N],
                     rhs=picked[z][:, cols].bitcast(FP8X4),
-                    rhs_scale=picked_scales[4 * z : P, cols],
+                    rhs_scale=planes[:, z * S + h * BANK : z * S + (h + 1) * BANK],
                     start=(z == 0),
                     stop=(z == PASSES - 1),
                 )
-            nc.vector.tensor_tensor(new[:, cols], acc[:], old[:, cols], mybir.AluOpType.min)
+        for h in range(S // BANK):
+            cols = slice(h * BANK, (h + 1) * BANK)
+            nc.vector.tensor_tensor(new[:, cols], acc[h][:], old[:, cols], mybir.AluOpType.min)
 
         nc.vector.tensor_copy(store[:].indirect(slot_sb[:]), new[:])
         nc.sync.dma_start(out, store[:])

@@ -17,6 +17,7 @@ P = 128
 PACK = 4
 PASSES = K // (P * PACK)
 BANK = 512
+SPLIT = 640
 
 
 def tile_picked_idxput_min_p_kernel(tc, x_words, x_scales, mem, w1, offs, slot, out):
@@ -30,47 +31,49 @@ def tile_picked_idxput_min_p_kernel(tc, x_words, x_scales, mem, w1, offs, slot, 
         scales = keep.tile([P, T], U8, name="scales", align_bytes=64)
         words = [keep.tile([P, T], I32, name=f"words{z}", align_bytes=64) for z in range(PASSES)]
         store = keep.tile([P, U], F32, name="store", align_bytes=64)
-        w_raw = [keep.tile([P, PACK, N], F32, name=f"w_raw{z}", align_bytes=64) for z in range(PASSES)]
+        w_first = keep.tile([P, PACK * N], F32, name="w_first", align_bytes=64)
+        old = keep.tile([P, SPLIT + PACK * N], F32, name="old", align_bytes=64)
+        w_raw = [t.rearrange("p (j n) -> p j n", j=PACK) for t in (w_first[:], old[:, SPLIT:])]
 
-        nc.vector.memset(scales[:].bitcast(I32), 0)
+        for first, last in ((32, 64), (64, P)):
+            nc.vector.memset(scales[first:last, :].bitcast(I32), 0)
         planes = keep.tile([P, PASSES * S], U8, name="planes", align_bytes=64)
         nc.vector.memset(planes[:].bitcast(I32), 0)
         nc.sync.dma_start(offs_sb[:], offs)
-        nc.sync.dma_start(slot_sb[:], slot)
-        nc.sync.dma_start(w_raw[0][:], w1[0:512, :].rearrange("(p j) n -> p j n", j=PACK))
         nc.sync.dma_start(
-            scales[0:P:4, :].bitcast(I32), x_scales.rearrange("z g c -> g z c").bitcast(I32)
+            scales[0:32, :].bitcast(I32), x_scales.rearrange("z g c -> g z c").bitcast(I32)
         )
+        nc.sync.dma_start(slot_sb[:], slot)
         for z in range(PASSES):
             nc.sync.dma_start(words[z][:], x_words[z].rearrange("p n t -> p (n t)").bitcast(I32))
-        nc.sync.dma_start(w_raw[1][:], w1[512:1024, :].rearrange("(p j) n -> p j n", j=PACK))
+        nc.sync.dma_start(w_raw[0], w1[0:512, :].rearrange("(p j) n -> p j n", j=PACK))
         nc.sync.dma_start(store[:], mem)
+        nc.sync.dma_start(w_raw[1], w1[512:1024, :].rearrange("(p j) n -> p j n", j=PACK))
 
-        w_bf = keep.tile([P, PASSES, N, PACK], BF16, name="w_bf", align_bytes=64)
+        w_bf = [keep.tile([P, N, PACK], BF16, name=f"w_bf{z}", align_bytes=64) for z in range(PASSES)]
+        w_codes = [keep.tile([P, N], U32, name=f"w_codes{z}", align_bytes=64) for z in range(PASSES)]
+        w_scales = [keep.tile([P, N], U8, name=f"w_scales{z}", align_bytes=64) for z in range(PASSES)]
         for z in range(PASSES):
-            nc.scalar.copy(w_bf[:, z], w_raw[z][:].rearrange("p j n -> p n j"))
+            nc.scalar.copy(w_bf[z][:], w_raw[z].rearrange("p j n -> p n j"))
 
         picked_scales = keep.tile([P, S], U8, name="picked_scales", align_bytes=64)
         nc.vector.tensor_copy(picked_scales[:], scales[:].indirect(offs_sb[:]))
         for q in range(4):
             nc.scalar.dma_start(
                 planes[32 * q : 32 * q + 4, :].bitcast(I32).rearrange("r (z c) -> r z c", z=PASSES),
-                picked_scales[32 * q : 32 * q + 32 : 4, :].bitcast(I32),
+                picked_scales[8 * q : 8 * q + 8, :].bitcast(I32),
             )
         picked = [keep.tile([P, S], U32, name=f"picked{z}", align_bytes=64) for z in range(PASSES)]
         for z in range(PASSES):
             nc.vector.tensor_copy(picked[z][:], words[z][:].bitcast(U32).indirect(offs_sb[:]))
+            nc.vector.quantize_mx(
+                out=w_codes[z][:].bitcast(FP8X4),
+                scales=w_scales[z][:],
+                in_=w_bf[z][:].rearrange("p n j -> p (n j)"),
+            )
 
-        w_codes = keep.tile([P, PASSES * N], U32, name="w_codes", align_bytes=64)
-        w_scales = keep.tile([P, PASSES * N], U8, name="w_scales", align_bytes=64)
-        nc.vector.quantize_mx(
-            out=w_codes[:].bitcast(FP8X4),
-            scales=w_scales[:],
-            in_=w_bf[:].rearrange("p z n j -> p (z n j)"),
-        )
-
-        old = keep.tile([P, S], F32, name="old", align_bytes=64)
-        nc.vector.tensor_copy(old[:], store[:].indirect(slot_sb[:]))
+        for a, b in ((0, SPLIT), (SPLIT, S)):
+            nc.vector.tensor_copy(old[:, a:b], store[:].indirect(slot_sb[:, a // 16 : b // 16]))
 
         new = keep.tile([P, S], F32, name="new", align_bytes=64)
         acc = [psum.tile([P, BANK], F32, name=f"acc{h}") for h in range(S // BANK)]
@@ -79,8 +82,8 @@ def tile_picked_idxput_min_p_kernel(tc, x_words, x_scales, mem, w1, offs, slot, 
                 cols = slice(h * BANK, (h + 1) * BANK)
                 nc.tensor.matmul_mx(
                     out=acc[h][:],
-                    lhsT=w_codes[:, z * N : (z + 1) * N].bitcast(FP8X4),
-                    lhsT_scale=w_scales[:, z * N : (z + 1) * N],
+                    lhsT=w_codes[z][:].bitcast(FP8X4),
+                    lhsT_scale=w_scales[z][:],
                     rhs=picked[z][:, cols].bitcast(FP8X4),
                     rhs_scale=planes[:, z * S + h * BANK : z * S + (h + 1) * BANK],
                     start=(z == 0),

@@ -54,7 +54,10 @@ def tile_picked_idxput_min_p_kernel(tc, x_words, x_scales, mem, w1, offs, slot, 
         w_codes = [keep.tile([P, N], U32, name=f"w_codes{z}", align_bytes=64) for z in range(PASSES)]
         w_scales = [keep.tile([P, N], U8, name=f"w_scales{z}", align_bytes=64) for z in range(PASSES)]
         for z in range(PASSES):
-            nc.scalar.copy(w_bf[z][:], w_raw[z].rearrange("p j n -> p n j"))
+            nc.scalar.copy(
+                w_bf[z][:].rearrange("p (c i) j -> p c j i", i=4),
+                w_raw[z].rearrange("p j (c i) -> p c j i", i=4),
+            )
 
         picked_scales = keep.tile([P, S], U8, name="picked_scales", align_bytes=64)
         nc.vector.tensor_copy(picked_scales[:], scales[:].indirect(offs_sb[:]))

@@ -16,7 +16,7 @@ FP8X4 = mybir.dt.float8_e4m3fn_x4
 P = 128
 PACK = 4
 PASSES = K // (P * PACK)
-BANK = 512
+BANK = 256
 SPLIT = 640
 
 
@@ -43,9 +43,9 @@ def tile_picked_idxput_min_p_kernel(tc, x_words, x_scales, mem, w1, offs, slot, 
         nc.sync.dma_start(
             scales[0:32, :].bitcast(I32), x_scales.rearrange("z g c -> g z c").bitcast(I32)
         )
-        nc.sync.dma_start(slot_sb[:], slot)
         for z in range(PASSES):
             nc.sync.dma_start(words[z][:], x_words[z].rearrange("p n t -> p (n t)").bitcast(I32))
+        nc.sync.dma_start(slot_sb[:], slot)
         nc.sync.dma_start(w_raw[0], w1[0:512, :].rearrange("(p j) n -> p j n", j=PACK))
         nc.sync.dma_start(store[:], mem)
         nc.sync.dma_start(w_raw[1], w1[512:1024, :].rearrange("(p j) n -> p j n", j=PACK))
@@ -62,7 +62,7 @@ def tile_picked_idxput_min_p_kernel(tc, x_words, x_scales, mem, w1, offs, slot, 
         picked_scales = keep.tile([P, S], U8, name="picked_scales", align_bytes=64)
         nc.vector.tensor_copy(picked_scales[:], scales[:].indirect(offs_sb[:]))
         for q in range(4):
-            nc.scalar.dma_start(
+            nc.sync.dma_start(
                 planes[32 * q : 32 * q + 4, :].bitcast(I32).rearrange("r (z c) -> r z c", z=PASSES),
                 picked_scales[8 * q : 8 * q + 8, :].bitcast(I32),
             )

@@ -12,12 +12,13 @@ U32 = mybir.dt.uint32
 U16 = mybir.dt.uint16
 U8 = mybir.dt.uint8
 FP8X4 = mybir.dt.float8_e4m3fn_x4
+ALU = mybir.AluOpType
 
 P = 128
 PACK = 4
 PASSES = K // (P * PACK)
-BANK = 256
-SPLIT = 640
+PARTS = ((128, 256), (256,), (128, 256))
+EARLY = 3
 
 
 def tile_picked_idxput_min_p_kernel(tc, x_words, x_scales, mem, w1, offs, slot, out):
@@ -31,9 +32,19 @@ def tile_picked_idxput_min_p_kernel(tc, x_words, x_scales, mem, w1, offs, slot, 
         scales = keep.tile([P, T], U8, name="scales", align_bytes=64)
         words = [keep.tile([P, T], I32, name=f"words{z}", align_bytes=64) for z in range(PASSES)]
         store = keep.tile([P, U], F32, name="store", align_bytes=64)
-        w_first = keep.tile([P, PACK * N], F32, name="w_first", align_bytes=64)
-        old = keep.tile([P, SPLIT + PACK * N], F32, name="old", align_bytes=64)
-        w_raw = [t.rearrange("p (j n) -> p j n", j=PACK) for t in (w_first[:], old[:, SPLIT:])]
+        staged = [keep.tile([P, PACK * N], F32, name=f"staged{z}", align_bytes=64) for z in range(PASSES)]
+        old_first = keep.tile([P, sum(PARTS[0])], F32, name="old_first", align_bytes=64)
+        w_raw = [t[:].rearrange("p (j n) -> p j n", j=PACK) for t in staged]
+        homes = [old_first, staged[0], staged[1]]
+        groups = []
+        part_start = []
+        at = 0
+        for home, widths in zip(homes, PARTS):
+            part_start.append(at)
+            for width in widths:
+                local = at - part_start[-1]
+                groups.append((slice(at, at + width), home[:, local : local + width]))
+                at = at + width
 
         for first, last in ((32, 64), (64, P)):
             nc.vector.memset(scales[first:last, :].bitcast(I32), 0)
@@ -46,9 +57,9 @@ def tile_picked_idxput_min_p_kernel(tc, x_words, x_scales, mem, w1, offs, slot, 
         for z in range(PASSES):
             nc.sync.dma_start(words[z][:], x_words[z].rearrange("p n t -> p (n t)").bitcast(I32))
         nc.sync.dma_start(slot_sb[:], slot)
-        nc.sync.dma_start(w_raw[0], w1[0:512, :].rearrange("(p j) n -> p j n", j=PACK))
         nc.sync.dma_start(store[:], mem)
-        nc.sync.dma_start(w_raw[1], w1[512:1024, :].rearrange("(p j) n -> p j n", j=PACK))
+        for z in range(PASSES):
+            nc.sync.dma_start(w_raw[z], w1[512 * z : 512 * (z + 1), :].rearrange("(p j) n -> p j n", j=PACK))
 
         w_bf = [keep.tile([P, N, PACK], BF16, name=f"w_bf{z}", align_bytes=64) for z in range(PASSES)]
         w_codes = [keep.tile([P, N], U32, name=f"w_codes{z}", align_bytes=64) for z in range(PASSES)]
@@ -69,32 +80,48 @@ def tile_picked_idxput_min_p_kernel(tc, x_words, x_scales, mem, w1, offs, slot, 
         picked = [keep.tile([P, S], U32, name=f"picked{z}", align_bytes=64) for z in range(PASSES)]
         for z in range(PASSES):
             nc.vector.tensor_copy(picked[z][:], words[z][:].bitcast(U32).indirect(offs_sb[:]))
+
+        def look_up(part):
+            a, width = part_start[part], sum(PARTS[part])
+            nc.vector.tensor_copy(homes[part][:, :width], store[:].indirect(slot_sb[:, a // 16 : (a + width) // 16]))
+
+        look_up(0)
+        for z in range(PASSES):
             nc.vector.quantize_mx(
                 out=w_codes[z][:].bitcast(FP8X4),
                 scales=w_scales[z][:],
                 in_=w_bf[z][:].rearrange("p n j -> p (n j)"),
             )
-
-        for a, b in ((0, SPLIT), (SPLIT, S)):
-            nc.vector.tensor_copy(old[:, a:b], store[:].indirect(slot_sb[:, a // 16 : b // 16]))
+            look_up(z + 1)
 
         new = keep.tile([P, S], F32, name="new", align_bytes=64)
-        acc = [psum.tile([P, BANK], F32, name=f"acc{h}") for h in range(S // BANK)]
-        for z in range(PASSES):
-            for h in range(S // BANK):
-                cols = slice(h * BANK, (h + 1) * BANK)
-                nc.tensor.matmul_mx(
-                    out=acc[h][:],
-                    lhsT=w_codes[z][:].bitcast(FP8X4),
-                    lhsT_scale=w_scales[z][:],
-                    rhs=picked[z][:, cols].bitcast(FP8X4),
-                    rhs_scale=planes[:, z * S + h * BANK : z * S + (h + 1) * BANK],
-                    start=(z == 0),
-                    stop=(z == PASSES - 1),
-                )
-        for h in range(S // BANK):
-            cols = slice(h * BANK, (h + 1) * BANK)
-            nc.vector.tensor_tensor(new[:, cols], acc[h][:], old[:, cols], mybir.AluOpType.min)
+        acc = [psum.tile([P, cols.stop - cols.start], F32, name=f"acc{cols.start}") for cols, old in groups]
+        for run in (range(EARLY), range(EARLY, len(groups))):
+            for z in range(PASSES):
+                for g in run:
+                    cols = groups[g][0]
+                    nc.tensor.matmul_mx(
+                        out=acc[g][:],
+                        lhsT=w_codes[z][:].bitcast(FP8X4),
+                        lhsT_scale=w_scales[z][:],
+                        rhs=picked[z][:, cols].bitcast(FP8X4),
+                        rhs_scale=planes[:, z * S + cols.start : z * S + cols.stop],
+                        start=(z == 0),
+                        stop=(z == PASSES - 1),
+                    )
 
-        nc.vector.tensor_copy(store[:].indirect(slot_sb[:]), new[:])
+        def smaller(g):
+            cols, old = groups[g]
+            nc.vector.tensor_tensor(new[:, cols], acc[g][:], old, ALU.min)
+
+        def put(a, b):
+            nc.vector.tensor_copy(store[:].indirect(slot_sb[:, a // 16 : b // 16]), new[:, a:b])
+
+        cut = groups[EARLY - 1][0].start
+        for g in range(EARLY):
+            smaller(g)
+        put(0, cut)
+        for g in range(EARLY, len(groups)):
+            smaller(g)
+        put(cut, S)
         nc.sync.dma_start(out, store[:])

@@ -17,8 +17,11 @@ ALU = mybir.AluOpType
 P = 128
 PACK = 4
 PASSES = K // (P * PACK)
-PARTS = ((128, 256), (256,), (128, 256))
-EARLY = 3
+STAGE = PACK * N
+FIRST, SECOND = 384, 256
+EARLY_GROUPS = (128, 128, 128)
+LATE_GROUPS = (512, 128)
+FIRST_PUT = 256
 
 
 def tile_picked_idxput_min_p_kernel(tc, x_words, x_scales, mem, w1, offs, slot, out):
@@ -32,19 +35,13 @@ def tile_picked_idxput_min_p_kernel(tc, x_words, x_scales, mem, w1, offs, slot, 
         scales = keep.tile([P, T], U8, name="scales", align_bytes=64)
         words = [keep.tile([P, T], I32, name=f"words{z}", align_bytes=64) for z in range(PASSES)]
         store = keep.tile([P, U], F32, name="store", align_bytes=64)
-        staged = [keep.tile([P, PACK * N], F32, name=f"staged{z}", align_bytes=64) for z in range(PASSES)]
-        old_first = keep.tile([P, sum(PARTS[0])], F32, name="old_first", align_bytes=64)
-        w_raw = [t[:].rearrange("p (j n) -> p j n", j=PACK) for t in staged]
-        homes = [old_first, staged[0], staged[1]]
-        groups = []
-        part_start = []
-        at = 0
-        for home, widths in zip(homes, PARTS):
-            part_start.append(at)
-            for width in widths:
-                local = at - part_start[-1]
-                groups.append((slice(at, at + width), home[:, local : local + width]))
-                at = at + width
+        staged = keep.tile([P, PASSES * STAGE], F32, name="staged", align_bytes=64)
+        old_early = keep.tile([P, FIRST], F32, name="old_early", align_bytes=64)
+        w_raw = [staged[:, z * STAGE : (z + 1) * STAGE].rearrange("p (j n) -> p j n", j=PACK) for z in range(PASSES)]
+        shift = STAGE - SECOND - FIRST
+
+        def old(a, b):
+            return old_early[:, a:b] if b <= FIRST else staged[:, a + shift : b + shift]
 
         for first, last in ((32, 64), (64, P)):
             nc.vector.memset(scales[first:last, :].bitcast(I32), 0)
@@ -72,7 +69,7 @@ def tile_picked_idxput_min_p_kernel(tc, x_words, x_scales, mem, w1, offs, slot, 
 
         picked_scales = keep.tile([P, S], U8, name="picked_scales", align_bytes=64)
         nc.vector.tensor_copy(picked_scales[:], scales[:].indirect(offs_sb[:]))
-        for q in range(4):
+        for q in (0, 2, 1, 3):
             nc.sync.dma_start(
                 planes[32 * q : 32 * q + 4, :].bitcast(I32).rearrange("r (z c) -> r z c", z=PASSES),
                 picked_scales[8 * q : 8 * q + 8, :].bitcast(I32),
@@ -81,47 +78,45 @@ def tile_picked_idxput_min_p_kernel(tc, x_words, x_scales, mem, w1, offs, slot, 
         for z in range(PASSES):
             nc.vector.tensor_copy(picked[z][:], words[z][:].bitcast(U32).indirect(offs_sb[:]))
 
-        def look_up(part):
-            a, width = part_start[part], sum(PARTS[part])
-            nc.vector.tensor_copy(homes[part][:, :width], store[:].indirect(slot_sb[:, a // 16 : (a + width) // 16]))
+        def look_up(a, b):
+            nc.vector.tensor_copy(old(a, b), store[:].indirect(slot_sb[:, a // 16 : b // 16]))
 
-        look_up(0)
+        borders = (0, FIRST, FIRST + SECOND, S)
+        look_up(borders[0], borders[1])
         for z in range(PASSES):
             nc.vector.quantize_mx(
                 out=w_codes[z][:].bitcast(FP8X4),
                 scales=w_scales[z][:],
                 in_=w_bf[z][:].rearrange("p n j -> p (n j)"),
             )
-            look_up(z + 1)
+            look_up(borders[z + 1], borders[z + 2])
 
         new = keep.tile([P, S], F32, name="new", align_bytes=64)
-        acc = [psum.tile([P, cols.stop - cols.start], F32, name=f"acc{cols.start}") for cols, old in groups]
-        for run in (range(EARLY), range(EARLY, len(groups))):
+
+        def project(start, widths):
+            groups = []
+            for width in widths:
+                groups.append((start, start + width, psum.tile([P, width], F32, name=f"acc{start}")))
+                start = start + width
             for z in range(PASSES):
-                for g in run:
-                    cols = groups[g][0]
+                for a, b, acc in groups:
                     nc.tensor.matmul_mx(
-                        out=acc[g][:],
+                        out=acc[:],
                         lhsT=w_codes[z][:].bitcast(FP8X4),
                         lhsT_scale=w_scales[z][:],
-                        rhs=picked[z][:, cols].bitcast(FP8X4),
-                        rhs_scale=planes[:, z * S + cols.start : z * S + cols.stop],
+                        rhs=picked[z][:, a:b].bitcast(FP8X4),
+                        rhs_scale=planes[:, z * S + a : z * S + b],
                         start=(z == 0),
                         stop=(z == PASSES - 1),
                     )
-
-        def smaller(g):
-            cols, old = groups[g]
-            nc.vector.tensor_tensor(new[:, cols], acc[g][:], old, ALU.min)
+            for a, b, acc in groups:
+                nc.vector.tensor_tensor(new[:, a:b], acc[:], old(a, b), ALU.min)
 
         def put(a, b):
             nc.vector.tensor_copy(store[:].indirect(slot_sb[:, a // 16 : b // 16]), new[:, a:b])
 
-        cut = groups[EARLY - 1][0].start
-        for g in range(EARLY):
-            smaller(g)
-        put(0, cut)
-        for g in range(EARLY, len(groups)):
-            smaller(g)
-        put(cut, S)
+        project(0, EARLY_GROUPS)
+        put(0, FIRST_PUT)
+        project(FIRST, LATE_GROUPS)
+        put(FIRST_PUT, S)
         nc.sync.dma_start(out, store[:])

@@ -18,10 +18,10 @@ P = 128
 PACK = 4
 PASSES = K // (P * PACK)
 STAGE = PACK * N
-FIRST, SECOND = 384, 256
-EARLY_GROUPS = (128, 128, 128)
-LATE_GROUPS = (512, 128)
-FIRST_PUT = 256
+FIRST = 640
+EARLY_GROUPS = (128, 256, 256)
+LATE_GROUPS = (256, 128)
+FIRST_PUT = 384
 
 
 def tile_picked_idxput_min_p_kernel(tc, x_words, x_scales, mem, w1, offs, slot, out):
@@ -35,13 +35,12 @@ def tile_picked_idxput_min_p_kernel(tc, x_words, x_scales, mem, w1, offs, slot, 
         scales = keep.tile([P, T], U8, name="scales", align_bytes=64)
         words = [keep.tile([P, T], I32, name=f"words{z}", align_bytes=64) for z in range(PASSES)]
         store = keep.tile([P, U], F32, name="store", align_bytes=64)
-        staged = keep.tile([P, PASSES * STAGE], F32, name="staged", align_bytes=64)
+        staged = [keep.tile([P, STAGE], F32, name=f"staged{z}", align_bytes=64) for z in range(PASSES)]
         old_early = keep.tile([P, FIRST], F32, name="old_early", align_bytes=64)
-        w_raw = [staged[:, z * STAGE : (z + 1) * STAGE].rearrange("p (j n) -> p j n", j=PACK) for z in range(PASSES)]
-        shift = STAGE - SECOND - FIRST
+        w_raw = [staged[z][:].rearrange("p (j n) -> p j n", j=PACK) for z in range(PASSES)]
 
         def old(a, b):
-            return old_early[:, a:b] if b <= FIRST else staged[:, a + shift : b + shift]
+            return old_early[:, a:b] if b <= FIRST else staged[1][:, a - FIRST : b - FIRST]
 
         for first, last in ((32, 64), (64, P)):
             nc.vector.memset(scales[first:last, :].bitcast(I32), 0)
@@ -53,10 +52,14 @@ def tile_picked_idxput_min_p_kernel(tc, x_words, x_scales, mem, w1, offs, slot, 
         )
         for z in range(PASSES):
             nc.sync.dma_start(words[z][:], x_words[z].rearrange("p n t -> p (n t)").bitcast(I32))
+
+        def load_weights(z):
+            nc.sync.dma_start(w_raw[z], w1[512 * z : 512 * (z + 1), :].rearrange("(p j) n -> p j n", j=PACK))
+
+        load_weights(0)
         nc.sync.dma_start(slot_sb[:], slot)
         nc.sync.dma_start(store[:], mem)
-        for z in range(PASSES):
-            nc.sync.dma_start(w_raw[z], w1[512 * z : 512 * (z + 1), :].rearrange("(p j) n -> p j n", j=PACK))
+        load_weights(1)
 
         w_bf = [keep.tile([P, N, PACK], BF16, name=f"w_bf{z}", align_bytes=64) for z in range(PASSES)]
         w_codes = [keep.tile([P, N], U32, name=f"w_codes{z}", align_bytes=64) for z in range(PASSES)]
@@ -69,7 +72,7 @@ def tile_picked_idxput_min_p_kernel(tc, x_words, x_scales, mem, w1, offs, slot, 
 
         picked_scales = keep.tile([P, S], U8, name="picked_scales", align_bytes=64)
         nc.vector.tensor_copy(picked_scales[:], scales[:].indirect(offs_sb[:]))
-        for q in (0, 2, 1, 3):
+        for q in range(4):
             nc.sync.dma_start(
                 planes[32 * q : 32 * q + 4, :].bitcast(I32).rearrange("r (z c) -> r z c", z=PASSES),
                 picked_scales[8 * q : 8 * q + 8, :].bitcast(I32),
@@ -81,42 +84,45 @@ def tile_picked_idxput_min_p_kernel(tc, x_words, x_scales, mem, w1, offs, slot, 
         def look_up(a, b):
             nc.vector.tensor_copy(old(a, b), store[:].indirect(slot_sb[:, a // 16 : b // 16]))
 
-        borders = (0, FIRST, FIRST + SECOND, S)
-        look_up(borders[0], borders[1])
+        borders = (0, FIRST, S)
         for z in range(PASSES):
             nc.vector.quantize_mx(
                 out=w_codes[z][:].bitcast(FP8X4),
                 scales=w_scales[z][:],
                 in_=w_bf[z][:].rearrange("p n j -> p (n j)"),
             )
-            look_up(borders[z + 1], borders[z + 2])
+            look_up(borders[z], borders[z + 1])
 
         new = keep.tile([P, S], F32, name="new", align_bytes=64)
 
-        def project(start, widths):
-            groups = []
-            for width in widths:
-                groups.append((start, start + width, psum.tile([P, width], F32, name=f"acc{start}")))
-                start = start + width
-            for z in range(PASSES):
-                for a, b, acc in groups:
-                    nc.tensor.matmul_mx(
-                        out=acc[:],
-                        lhsT=w_codes[z][:].bitcast(FP8X4),
-                        lhsT_scale=w_scales[z][:],
-                        rhs=picked[z][:, a:b].bitcast(FP8X4),
-                        rhs_scale=planes[:, z * S + a : z * S + b],
-                        start=(z == 0),
-                        stop=(z == PASSES - 1),
-                    )
-            for a, b, acc in groups:
-                nc.vector.tensor_tensor(new[:, a:b], acc[:], old(a, b), ALU.min)
+        def multiply(acc, a, b, z):
+            nc.tensor.matmul_mx(
+                out=acc,
+                lhsT=w_codes[z][:].bitcast(FP8X4),
+                lhsT_scale=w_scales[z][:],
+                rhs=picked[z][:, a:b].bitcast(FP8X4),
+                rhs_scale=planes[:, z * S + a : z * S + b],
+                start=(z == 0),
+                stop=(z == PASSES - 1),
+            )
+
+        def spans(start, widths):
+            return [(start + sum(widths[:g]), start + sum(widths[: g + 1])) for g in range(len(widths))]
 
         def put(a, b):
             nc.vector.tensor_copy(store[:].indirect(slot_sb[:, a // 16 : b // 16]), new[:, a:b])
 
-        project(0, EARLY_GROUPS)
+        early = [(a, b, psum.tile([P, b - a], F32, name=f"acc{a}")) for a, b in spans(0, EARLY_GROUPS)]
+        for z in range(PASSES):
+            for a, b, acc in early:
+                multiply(acc[:], a, b, z)
+        for a, b, acc in early:
+            nc.vector.tensor_tensor(new[:, a:b], acc[:], old(a, b), ALU.min)
         put(0, FIRST_PUT)
-        project(FIRST, LATE_GROUPS)
+        late = psum.tile([P, S - FIRST], F32, name="late")
+        for a, b in spans(FIRST, LATE_GROUPS):
+            for z in range(PASSES):
+                multiply(late[:, a - FIRST : b - FIRST], a, b, z)
+        nc.vector.tensor_tensor(new[:, FIRST:S], late[:], old(FIRST, S), ALU.min)
         put(FIRST_PUT, S)
         nc.sync.dma_start(out, store[:])

@@ -124,5 +124,6 @@ def tile_picked_idxput_min_p_kernel(tc, x_words, x_scales, mem, w1, offs, slot, 
             for z in range(PASSES):
                 multiply(late[:, a - FIRST : b - FIRST], a, b, z)
         nc.vector.tensor_tensor(new[:, FIRST:S], late[:], old(FIRST, S), ALU.min)
+        nc.sync.dma_start(out[:, 0:64], new[:, S - 64 : S])
         put(FIRST_PUT, S)
         nc.sync.dma_start(out, store[:])

@@ -46,10 +46,10 @@ def tile_picked_idxput_min_p_kernel(tc, x_words, x_scales, mem, w1, offs, slot, 
             nc.vector.memset(scales[first:last, :].bitcast(I32), 0)
         planes = keep.tile([P, PASSES * S], U8, name="planes", align_bytes=64)
         nc.vector.memset(planes[:].bitcast(I32), 0)
-        nc.sync.dma_start(offs_sb[:], offs)
         nc.sync.dma_start(
             scales[0:32, :].bitcast(I32), x_scales.rearrange("z g c -> g z c").bitcast(I32)
         )
+        nc.sync.dma_start(offs_sb[:], offs)
         for z in range(PASSES):
             nc.sync.dma_start(words[z][:], x_words[z].rearrange("p n t -> p (n t)").bitcast(I32))
 

@@ -13,15 +13,17 @@ U16 = mybir.dt.uint16
 U8 = mybir.dt.uint8
 FP8X4 = mybir.dt.float8_e4m3fn_x4
 ALU = mybir.AluOpType
+ACT = mybir.ActivationFunctionType
 
 P = 128
 PACK = 4
 PASSES = K // (P * PACK)
-STAGE = PACK * N
-FIRST = 640
-EARLY_GROUPS = (128, 256, 256)
-LATE_GROUPS = (256, 128)
-FIRST_PUT = 384
+GROUP = 256
+EARLY = 512
+LOOK_VECTOR = ((0, 256), (256, 384))
+LOOK_SCALAR = ((384, 768), (768, S))
+PIECES = ((0, 256), (256, 768), (768, S))
+CHUNKS = (256, 512, 512, 512, 256)
 
 
 def tile_picked_idxput_min_p_kernel(tc, x_words, x_scales, mem, w1, offs, slot, out):
@@ -34,96 +36,110 @@ def tile_picked_idxput_min_p_kernel(tc, x_words, x_scales, mem, w1, offs, slot, 
         slot_sb = keep.tile([P, S // 16], U16, name="slot_sb")
         scales = keep.tile([P, T], U8, name="scales", align_bytes=64)
         words = [keep.tile([P, T], I32, name=f"words{z}", align_bytes=64) for z in range(PASSES)]
-        store = keep.tile([P, U], F32, name="store", align_bytes=64)
-        staged = [keep.tile([P, STAGE], F32, name=f"staged{z}", align_bytes=64) for z in range(PASSES)]
-        old_early = keep.tile([P, FIRST], F32, name="old_early", align_bytes=64)
-        w_raw = [staged[z][:].rearrange("p (j n) -> p j n", j=PACK) for z in range(PASSES)]
-
-        def old(a, b):
-            return old_early[:, a:b] if b <= FIRST else staged[1][:, a - FIRST : b - FIRST]
-
-        for first, last in ((32, 64), (64, P)):
-            nc.vector.memset(scales[first:last, :].bitcast(I32), 0)
-        planes = keep.tile([P, PASSES * S], U8, name="planes", align_bytes=64)
-        nc.vector.memset(planes[:].bitcast(I32), 0)
-        nc.sync.dma_start(
-            scales[0:32, :].bitcast(I32), x_scales.rearrange("z g c -> g z c").bitcast(I32)
-        )
-        nc.sync.dma_start(offs_sb[:], offs)
-        for z in range(PASSES):
-            nc.sync.dma_start(words[z][:], x_words[z].rearrange("p n t -> p (n t)").bitcast(I32))
-
-        def load_weights(z):
-            nc.sync.dma_start(w_raw[z], w1[512 * z : 512 * (z + 1), :].rearrange("(p j) n -> p j n", j=PACK))
-
-        load_weights(0)
-        nc.sync.dma_start(slot_sb[:], slot)
-        nc.sync.dma_start(store[:], mem)
-        load_weights(1)
-
+        store_s = keep.tile([P, U], F32, name="store_s", align_bytes=64)
+        store_v = keep.tile([P, U], F32, name="store_v", align_bytes=64)
+        w_raw = [keep.tile([P, PACK, N], F32, name=f"w_raw{z}", align_bytes=64) for z in range(PASSES)]
+        halves = ((0, EARLY), (EARLY, S))
+        planes = [keep.tile([P, PASSES, b - a], U8, name=f"planes{a}", align_bytes=64) for a, b in halves]
+        picked_scales = keep.tile([P, S], U8, name="picked_scales", align_bytes=64)
+        picked = [keep.tile([P, S], U32, name=f"picked{z}", align_bytes=64) for z in range(PASSES)]
         w_bf = [keep.tile([P, N, PACK], BF16, name=f"w_bf{z}", align_bytes=64) for z in range(PASSES)]
         w_codes = [keep.tile([P, N], U32, name=f"w_codes{z}", align_bytes=64) for z in range(PASSES)]
         w_scales = [keep.tile([P, N], U8, name=f"w_scales{z}", align_bytes=64) for z in range(PASSES)]
+        old = keep.tile([P, S], F32, name="old", align_bytes=64)
+        new = [keep.tile([P, b - a], F32, name=f"new{a}", align_bytes=64) for a, b in PIECES]
+        joined = keep.tile([P, U], F32, name="joined", align_bytes=64)
+
+        def load_weights(z):
+            nc.sync.dma_start(w_raw[z][:], w1[512 * z : 512 * (z + 1), :].rearrange("(p j) n -> p j n", j=PACK))
+
+        for first, last in ((32, 64), (64, P)):
+            nc.vector.memset(scales[first:last, :].bitcast(I32), 0)
+        for plane in planes:
+            nc.vector.memset(plane[:].bitcast(I32), 0)
+        nc.sync.dma_start(scales[0:32, :].bitcast(I32), x_scales.rearrange("z g c -> g z c").bitcast(I32))
+        nc.sync.dma_start(offs_sb[:], offs)
+        for z in range(PASSES):
+            if z > 0:
+                load_weights(z - 1)
+            nc.sync.dma_start(words[z][:], x_words[z].rearrange("p n t -> p (n t)").bitcast(I32))
+        load_weights(PASSES - 1)
+        nc.sync.dma_start(slot_sb[:], slot)
+
+        nc.vector.tensor_copy(picked_scales[:], scales[:].indirect(offs_sb[:]))
+
+        def place_scales(h):
+            a, b = halves[h]
+            for q in range(4):
+                nc.sync.dma_start(
+                    planes[h][32 * q : 32 * q + 4].bitcast(I32), picked_scales[8 * q : 8 * q + 8, a:b].bitcast(I32)
+                )
+
+        place_scales(0)
+        nc.sync.dma_start(store_s[:], mem)
+        place_scales(1)
+        nc.sync.dma_start(store_v[:], mem)
+
         for z in range(PASSES):
             nc.scalar.copy(
                 w_bf[z][:].rearrange("p (c i) j -> p c j i", i=4),
-                w_raw[z].rearrange("p j (c i) -> p c j i", i=4),
+                w_raw[z][:].rearrange("p j (c i) -> p c j i", i=4),
             )
 
-        picked_scales = keep.tile([P, S], U8, name="picked_scales", align_bytes=64)
-        nc.vector.tensor_copy(picked_scales[:], scales[:].indirect(offs_sb[:]))
-        for q in range(4):
-            nc.sync.dma_start(
-                planes[32 * q : 32 * q + 4, :].bitcast(I32).rearrange("r (z c) -> r z c", z=PASSES),
-                picked_scales[8 * q : 8 * q + 8, :].bitcast(I32),
-            )
-        picked = [keep.tile([P, S], U32, name=f"picked{z}", align_bytes=64) for z in range(PASSES)]
-        for z in range(PASSES):
+        def pick(z):
             nc.vector.tensor_copy(picked[z][:], words[z][:].bitcast(U32).indirect(offs_sb[:]))
 
-        def look_up(a, b):
-            nc.vector.tensor_copy(old(a, b), store[:].indirect(slot_sb[:, a // 16 : b // 16]))
-
-        borders = (0, FIRST, S)
-        for z in range(PASSES):
+        def quantise(z):
             nc.vector.quantize_mx(
                 out=w_codes[z][:].bitcast(FP8X4),
                 scales=w_scales[z][:],
                 in_=w_bf[z][:].rearrange("p n j -> p (n j)"),
             )
-            look_up(borders[z], borders[z + 1])
 
-        new = keep.tile([P, S], F32, name="new", align_bytes=64)
+        for z in range(PASSES):
+            pick(z)
+            quantise(z)
 
-        def multiply(acc, a, b, z):
+        accs = [psum.tile([P, b - a], F32, name=f"acc{a}") for a, b in PIECES]
+
+        def multiply(z, c):
+            g = [a <= c < b for a, b in PIECES].index(True)
+            a, b = PIECES[g]
+            h = c // EARLY
             nc.tensor.matmul_mx(
-                out=acc,
+                out=accs[g][:, c - a : c - a + GROUP],
                 lhsT=w_codes[z][:].bitcast(FP8X4),
                 lhsT_scale=w_scales[z][:],
-                rhs=picked[z][:, a:b].bitcast(FP8X4),
-                rhs_scale=planes[:, z * S + a : z * S + b],
-                start=(z == 0),
-                stop=(z == PASSES - 1),
+                rhs=picked[z][:, c : c + GROUP].bitcast(FP8X4),
+                rhs_scale=planes[h][:, z, c - halves[h][0] : c - halves[h][0] + GROUP],
+                start=(z == 0 and c == a),
+                stop=(z == PASSES - 1 and c + GROUP == b),
             )
 
-        def spans(start, widths):
-            return [(start + sum(widths[:g]), start + sum(widths[: g + 1])) for g in range(len(widths))]
-
-        def put(a, b):
-            nc.vector.tensor_copy(store[:].indirect(slot_sb[:, a // 16 : b // 16]), new[:, a:b])
-
-        early = [(a, b, psum.tile([P, b - a], F32, name=f"acc{a}")) for a, b in spans(0, EARLY_GROUPS)]
         for z in range(PASSES):
-            for a, b, acc in early:
-                multiply(acc[:], a, b, z)
-        for a, b, acc in early:
-            nc.vector.tensor_tensor(new[:, a:b], acc[:], old(a, b), ALU.min)
-        put(0, FIRST_PUT)
-        late = psum.tile([P, S - FIRST], F32, name="late")
-        for a, b in spans(FIRST, LATE_GROUPS):
+            for c in range(0, EARLY, GROUP):
+                multiply(z, c)
+        for c in range(EARLY, S, GROUP):
             for z in range(PASSES):
-                multiply(late[:, a - FIRST : b - FIRST], a, b, z)
-        nc.vector.tensor_tensor(new[:, FIRST:S], late[:], old(FIRST, S), ALU.min)
-        nc.sync.dma_start(out[:, 0:64], new[:, S - 64 : S])
-        put(FIRST_PUT, S)
-        nc.sync.dma_start(out, store[:])
+                multiply(z, c)
+
+        def places(window, a, b):
+            return window[:].indirect(slot_sb[:, a // 16 : b // 16])
+
+        for a, b in LOOK_VECTOR:
+            nc.vector.tensor_copy(old[:, a:b], places(store_s, a, b))
+        for a, b in LOOK_SCALAR:
+            nc.scalar.activation(old[:, a:b], places(store_s, a, b), ACT.Copy)
+        for (a, b), fresh, acc in zip(PIECES, new, accs):
+            nc.vector.tensor_tensor(fresh[:], acc[:], old[:, a:b], ALU.min)
+
+        nc.scalar.activation(places(store_s, *PIECES[0]), new[0][:], ACT.Copy)
+        nc.vector.tensor_copy(places(store_v, *PIECES[1]), new[1][:])
+        nc.scalar.activation(places(store_s, *PIECES[2]), new[2][:], ACT.Copy)
+
+        start = 0
+        for width in CHUNKS:
+            cols = slice(start, start + width)
+            nc.vector.tensor_tensor(joined[:, cols], store_s[:, cols], store_v[:, cols], ALU.min)
+            nc.sync.dma_start(out[:, cols], joined[:, cols])
+            start = start + width

@@ -19,6 +19,7 @@ P = 128
 PACK = 4
 PASSES = K // (P * PACK)
 GROUP = 256
+APART = 128 * 1024
 EARLY = 512
 LOOK_VECTOR = ((0, 256), (256, 384))
 LOOK_SCALAR = ((384, 768), (768, S))
@@ -30,6 +31,7 @@ def tile_picked_idxput_min_p_kernel(tc, x_words, x_scales, mem, w1, offs, slot, 
     nc = tc.nc
     with ExitStack() as ctx:
         keep = ctx.enter_context(tc.tile_pool(name="keep", bufs=1))
+        far = ctx.enter_context(tc.tile_pool(name="far", bufs=1))
         psum = ctx.enter_context(tc.psum_pool(name="psum", bufs=1))
 
         offs_sb = keep.tile([P, S // 16], U16, name="offs_sb")
@@ -37,7 +39,7 @@ def tile_picked_idxput_min_p_kernel(tc, x_words, x_scales, mem, w1, offs, slot, 
         scales = keep.tile([P, T], U8, name="scales", align_bytes=64)
         words = [keep.tile([P, T], I32, name=f"words{z}", align_bytes=64) for z in range(PASSES)]
         store_s = keep.tile([P, U], F32, name="store_s", align_bytes=64)
-        store_v = keep.tile([P, U], F32, name="store_v", align_bytes=64)
+        store_v = far.tile([P, U], F32, name="store_v", align_bytes=64, offset=APART)
         w_raw = [keep.tile([P, PACK, N], F32, name=f"w_raw{z}", align_bytes=64) for z in range(PASSES)]
         halves = ((0, EARLY), (EARLY, S))
         planes = [keep.tile([P, PASSES, b - a], U8, name=f"planes{a}", align_bytes=64) for a, b in halves]

@@ -20,11 +20,10 @@ PACK = 4
 PASSES = K // (P * PACK)
 GROUP = 256
 APART = 128 * 1024
-EARLY = 512
 LOOK_VECTOR = ((0, 256), (256, 384))
 LOOK_SCALAR = ((384, 768), (768, S))
 PIECES = ((0, 256), (256, 768), (768, S))
-CHUNKS = (256, 512, 512, 512, 256)
+CHUNKS = (448, 544, 544, 512)
 
 
 def tile_picked_idxput_min_p_kernel(tc, x_words, x_scales, mem, w1, offs, slot, out):
@@ -40,9 +39,8 @@ def tile_picked_idxput_min_p_kernel(tc, x_words, x_scales, mem, w1, offs, slot, 
         words = [keep.tile([P, T], I32, name=f"words{z}", align_bytes=64) for z in range(PASSES)]
         store_s = keep.tile([P, U], F32, name="store_s", align_bytes=64)
         store_v = far.tile([P, U], F32, name="store_v", align_bytes=64, offset=APART)
-        w_raw = [keep.tile([P, PACK, N], F32, name=f"w_raw{z}", align_bytes=64) for z in range(PASSES)]
-        halves = ((0, EARLY), (EARLY, S))
-        planes = [keep.tile([P, PASSES, b - a], U8, name=f"planes{a}", align_bytes=64) for a, b in halves]
+        w_raw = keep.tile([P, PASSES, PACK, N], F32, name="w_raw", align_bytes=64)
+        planes = keep.tile([P, PASSES, S], U8, name="planes", align_bytes=64)
         picked_scales = keep.tile([P, S], U8, name="picked_scales", align_bytes=64)
         picked = [keep.tile([P, S], U32, name=f"picked{z}", align_bytes=64) for z in range(PASSES)]
         w_bf = [keep.tile([P, N, PACK], BF16, name=f"w_bf{z}", align_bytes=64) for z in range(PASSES)]
@@ -52,40 +50,26 @@ def tile_picked_idxput_min_p_kernel(tc, x_words, x_scales, mem, w1, offs, slot, 
         new = [keep.tile([P, b - a], F32, name=f"new{a}", align_bytes=64) for a, b in PIECES]
         joined = keep.tile([P, U], F32, name="joined", align_bytes=64)
 
-        def load_weights(z):
-            nc.sync.dma_start(w_raw[z][:], w1[512 * z : 512 * (z + 1), :].rearrange("(p j) n -> p j n", j=PACK))
-
         for first, last in ((32, 64), (64, P)):
             nc.vector.memset(scales[first:last, :].bitcast(I32), 0)
-        for plane in planes:
-            nc.vector.memset(plane[:].bitcast(I32), 0)
+        nc.vector.memset(planes[:].bitcast(I32), 0)
         nc.sync.dma_start(scales[0:32, :].bitcast(I32), x_scales.rearrange("z g c -> g z c").bitcast(I32))
         nc.sync.dma_start(offs_sb[:], offs)
         for z in range(PASSES):
-            if z > 0:
-                load_weights(z - 1)
             nc.sync.dma_start(words[z][:], x_words[z].rearrange("p n t -> p (n t)").bitcast(I32))
-        load_weights(PASSES - 1)
+        nc.sync.dma_start(w_raw[:], w1.rearrange("(z p j) n -> p z j n", z=PASSES, j=PACK))
         nc.sync.dma_start(slot_sb[:], slot)
 
         nc.vector.tensor_copy(picked_scales[:], scales[:].indirect(offs_sb[:]))
-
-        def place_scales(h):
-            a, b = halves[h]
-            for q in range(4):
-                nc.sync.dma_start(
-                    planes[h][32 * q : 32 * q + 4].bitcast(I32), picked_scales[8 * q : 8 * q + 8, a:b].bitcast(I32)
-                )
-
-        place_scales(0)
+        for q in range(4):
+            nc.sync.dma_start(planes[32 * q : 32 * q + 4].bitcast(I32), picked_scales[8 * q : 8 * q + 8, :].bitcast(I32))
         nc.sync.dma_start(store_s[:], mem)
-        place_scales(1)
         nc.sync.dma_start(store_v[:], mem)
 
         for z in range(PASSES):
             nc.scalar.copy(
                 w_bf[z][:].rearrange("p (c i) j -> p c j i", i=4),
-                w_raw[z][:].rearrange("p j (c i) -> p c j i", i=4),
+                w_raw[:, z].rearrange("p j (c i) -> p c j i", i=4),
             )
 
         def pick(z):
@@ -100,6 +84,7 @@ def tile_picked_idxput_min_p_kernel(tc, x_words, x_scales, mem, w1, offs, slot, 
 
         for z in range(PASSES):
             pick(z)
+        for z in range(PASSES):
             quantise(z)
 
         accs = [psum.tile([P, b - a], F32, name=f"acc{a}") for a, b in PIECES]
@@ -107,21 +92,17 @@ def tile_picked_idxput_min_p_kernel(tc, x_words, x_scales, mem, w1, offs, slot, 
         def multiply(z, c):
             g = [a <= c < b for a, b in PIECES].index(True)
             a, b = PIECES[g]
-            h = c // EARLY
             nc.tensor.matmul_mx(
                 out=accs[g][:, c - a : c - a + GROUP],
                 lhsT=w_codes[z][:].bitcast(FP8X4),
                 lhsT_scale=w_scales[z][:],
                 rhs=picked[z][:, c : c + GROUP].bitcast(FP8X4),
-                rhs_scale=planes[h][:, z, c - halves[h][0] : c - halves[h][0] + GROUP],
+                rhs_scale=planes[:, z, c : c + GROUP],
                 start=(z == 0 and c == a),
                 stop=(z == PASSES - 1 and c + GROUP == b),
             )
 
-        for z in range(PASSES):
-            for c in range(0, EARLY, GROUP):
-                multiply(z, c)
-        for c in range(EARLY, S, GROUP):
+        for c in range(0, S, GROUP):
             for z in range(PASSES):
                 multiply(z, c)
 

@@ -19,6 +19,7 @@ P = 128
 PACK = 4
 PASSES = K // (P * PACK)
 GROUP = 256
+QUADRANTS = (0, 2, 1, 3)
 APART = 128 * 1024
 LOOK_VECTOR = ((0, 256), (256, 384))
 LOOK_SCALAR = ((384, 768), (768, S))
@@ -61,7 +62,7 @@ def tile_picked_idxput_min_p_kernel(tc, x_words, x_scales, mem, w1, offs, slot, 
         nc.sync.dma_start(slot_sb[:], slot)
 
         nc.vector.tensor_copy(picked_scales[:], scales[:].indirect(offs_sb[:]))
-        for q in range(4):
+        for q in QUADRANTS:
             nc.sync.dma_start(planes[32 * q : 32 * q + 4].bitcast(I32), picked_scales[8 * q : 8 * q + 8, :].bitcast(I32))
         nc.sync.dma_start(store_s[:], mem)
         nc.sync.dma_start(store_v[:], mem)

@@ -103,9 +103,10 @@ def tile_picked_idxput_min_p_kernel(tc, x_words, x_scales, mem, w1, offs, slot, 
                 stop=(z == PASSES - 1 and c + GROUP == b),
             )
 
-        for c in range(0, S, GROUP):
+        for first, last in ((0, PIECES[1][1]), PIECES[2]):
             for z in range(PASSES):
-                multiply(z, c)
+                for c in range(first, last, GROUP):
+                    multiply(z, c)
 
         def places(window, a, b):
             return window[:].indirect(slot_sb[:, a // 16 : b // 16])

from contextlib import ExitStack

import concourse.mybir as mybir

K, T, S, N, U = 1024, 2048, 1024, 128, 2048
FLOPS = 2 * K * S * N

F32 = mybir.dt.float32
BF16 = mybir.dt.bfloat16
I32 = mybir.dt.int32
U32 = mybir.dt.uint32
U16 = mybir.dt.uint16
U8 = mybir.dt.uint8
FP8X4 = mybir.dt.float8_e4m3fn_x4
ALU = mybir.AluOpType
ACT = mybir.ActivationFunctionType

P = 128
PACK = 4
PASSES = K // (P * PACK)
GROUP = 256
QUADRANTS = (0, 2, 1, 3)
APART = 128 * 1024
LOOK_VECTOR = ((0, 256), (256, 384))
LOOK_SCALAR = ((384, 768), (768, S))
PIECES = ((0, 256), (256, 768), (768, S))
CHUNKS = (448, 544, 544, 512)


def tile_picked_idxput_min_p_kernel(tc, x_words, x_scales, mem, w1, offs, slot, out):
    nc = tc.nc
    with ExitStack() as ctx:
        keep = ctx.enter_context(tc.tile_pool(name="keep", bufs=1))
        far = ctx.enter_context(tc.tile_pool(name="far", bufs=1))
        psum = ctx.enter_context(tc.psum_pool(name="psum", bufs=1))

        offs_sb = keep.tile([P, S // 16], U16, name="offs_sb")
        slot_sb = keep.tile([P, S // 16], U16, name="slot_sb")
        scales = keep.tile([P, T], U8, name="scales", align_bytes=64)
        words = [keep.tile([P, T], I32, name=f"words{z}", align_bytes=64) for z in range(PASSES)]
        store_s = keep.tile([P, U], F32, name="store_s", align_bytes=64)
        store_v = far.tile([P, U], F32, name="store_v", align_bytes=64, offset=APART)
        w_raw = keep.tile([P, PASSES, PACK, N], F32, name="w_raw", align_bytes=64)
        planes = keep.tile([P, PASSES, S], U8, name="planes", align_bytes=64)
        picked_scales = keep.tile([P, S], U8, name="picked_scales", align_bytes=64)
        picked = [keep.tile([P, S], U32, name=f"picked{z}", align_bytes=64) for z in range(PASSES)]
        w_bf = [keep.tile([P, N, PACK], BF16, name=f"w_bf{z}", align_bytes=64) for z in range(PASSES)]
        w_codes = [keep.tile([P, N], U32, name=f"w_codes{z}", align_bytes=64) for z in range(PASSES)]
        w_scales = [keep.tile([P, N], U8, name=f"w_scales{z}", align_bytes=64) for z in range(PASSES)]
        old = keep.tile([P, S], F32, name="old", align_bytes=64)
        new = [keep.tile([P, b - a], F32, name=f"new{a}", align_bytes=64) for a, b in PIECES]
        joined = keep.tile([P, U], F32, name="joined", align_bytes=64)

        for first, last in ((32, 64), (64, P)):
            nc.vector.memset(scales[first:last, :].bitcast(I32), 0)
        nc.vector.memset(planes[:].bitcast(I32), 0)
        nc.sync.dma_start(scales[0:32, :].bitcast(I32), x_scales.rearrange("z g c -> g z c").bitcast(I32))
        nc.sync.dma_start(offs_sb[:], offs)
        for z in range(PASSES):
            nc.sync.dma_start(words[z][:], x_words[z].rearrange("p n t -> p (n t)").bitcast(I32))
        nc.sync.dma_start(w_raw[:], w1.rearrange("(z p j) n -> p z j n", z=PASSES, j=PACK))
        nc.sync.dma_start(slot_sb[:], slot)

        nc.vector.tensor_copy(picked_scales[:], scales[:].indirect(offs_sb[:]))
        for q in QUADRANTS:
            nc.sync.dma_start(planes[32 * q : 32 * q + 4].bitcast(I32), picked_scales[8 * q : 8 * q + 8, :].bitcast(I32))
        nc.sync.dma_start(store_s[:], mem)
        nc.sync.dma_start(store_v[:], mem)

        for z in range(PASSES):
            nc.scalar.copy(
                w_bf[z][:].rearrange("p (c i) j -> p c j i", i=4),
                w_raw[:, z].rearrange("p j (c i) -> p c j i", i=4),
            )

        def pick(z):
            nc.vector.tensor_copy(picked[z][:], words[z][:].bitcast(U32).indirect(offs_sb[:]))

        def quantise(z):
            nc.vector.quantize_mx(
                out=w_codes[z][:].bitcast(FP8X4),
                scales=w_scales[z][:],
                in_=w_bf[z][:].rearrange("p n j -> p (n j)"),
            )

        for z in range(PASSES):
            pick(z)
        for z in range(PASSES):
            quantise(z)

        accs = [psum.tile([P, b - a], F32, name=f"acc{a}") for a, b in PIECES]

        def multiply(z, c):
            g = [a <= c < b for a, b in PIECES].index(True)
            a, b = PIECES[g]
            nc.tensor.matmul_mx(
                out=accs[g][:, c - a : c - a + GROUP],
                lhsT=w_codes[z][:].bitcast(FP8X4),
                lhsT_scale=w_scales[z][:],
                rhs=picked[z][:, c : c + GROUP].bitcast(FP8X4),
                rhs_scale=planes[:, z, c : c + GROUP],
                start=(z == 0 and c == a),
                stop=(z == PASSES - 1 and c + GROUP == b),
            )

        for first, last in ((0, PIECES[1][1]), PIECES[2]):
            for z in range(PASSES):
                for c in range(first, last, GROUP):
                    multiply(z, c)

        def places(window, a, b):
            return window[:].indirect(slot_sb[:, a // 16 : b // 16])

        for a, b in LOOK_VECTOR:
            nc.vector.tensor_copy(old[:, a:b], places(store_s, a, b))
        for a, b in LOOK_SCALAR:
            nc.scalar.activation(old[:, a:b], places(store_s, a, b), ACT.Copy)
        for (a, b), fresh, acc in zip(PIECES, new, accs):
            nc.vector.tensor_tensor(fresh[:], acc[:], old[:, a:b], ALU.min)

        nc.scalar.activation(places(store_s, *PIECES[0]), new[0][:], ACT.Copy)
        nc.vector.tensor_copy(places(store_v, *PIECES[1]), new[1][:])
        nc.scalar.activation(places(store_s, *PIECES[2]), new[2][:], ACT.Copy)

        start = 0
        for width in CHUNKS:
            cols = slice(start, start + width)
            nc.vector.tensor_tensor(joined[:, cols], store_s[:, cols], store_v[:, cols], ALU.min)
            nc.sync.dma_start(out[:, cols], joined[:, cols])
            start = start + width
